import numpy as np
CORES = [100,101,102,103,108,109,110,111]
N = 8
TIMES = 1
def setup_inputs(rng):
    x = (rng.standard_normal((N, 128, 128), dtype=np.float32) / np.float32(np.sqrt(512 * N)))
    return {"x": x, "xt": x.transpose(0, 2, 1).copy()}
def setup_inputs_big(rng):
    d = setup_inputs(rng)
    for k in ("x", "xt"): d[k] = (d[k].astype(np.float32) * 1024.0).astype(d[k].dtype)
    return d
def setup_inputs_small(rng):
    d = setup_inputs(rng)
    for k in ("x", "xt"): d[k] = (d[k].astype(np.float32) * (1 / 1024.0)).astype(d[k].dtype)
    return d
def setup_inputs_apart(rng):
    d = setup_inputs(rng)
    f = (10.0 ** rng.permutation(np.linspace(-1.5, 1.5, N))).astype(np.float32).reshape(N, 1, 1)
    for k in ("x", "xt"): d[k] = (d[k].astype(np.float32) * f).astype(d[k].dtype)
    return d
def reference(x, xt):
    X = list(x.astype(np.float64))
    for _ in range(TIMES):
        G = sum(a.T @ a for a in X)
        X = [1.5 * a - 0.5 * (a @ G) for a in X]
    return {"y": np.stack(X).astype(np.float32)}

@@ -1,0 +1,111 @@
+from concourse.bass import DstId, RemoteDMATransfer
+from concourse.mybir import AluOpType
+
+D = 128
+F32 = "float32"
+SCRATCH = {
+    "xs": ("sbuf", [D, D], F32),
+    "xts": ("sbuf", [D, D], F32),
+    "ch": ("sbuf", [D, D], F32),
+    "c15": ("sbuf", [D, D], F32),
+    "xth": ("sbuf", [D, D], F32),
+    "x15": ("sbuf", [D, D], F32),
+    "g0": ("sbuf", [D, D], F32),
+    "g1": ("sbuf", [D, D], F32),
+    "g2": ("sbuf", [D, D], F32),
+    "g3": ("sbuf", [D, D], F32),
+    "so": ("sbuf", [D, D], F32),
+    "ys": ("sbuf", [D, D], F32),
+    "gp": ("psum", [D, 512], F32),
+    "pp": ("psum", [D, 512], F32),
+}
+SEMAPHORES = ["ld_x", "ld_xt", "ms", "s_g", "s_gs", "s_xth", "s_x15", "s_p", "s_y", "st",
+              "arr0", "arr1", "arr2", "arr3", "arr_x", "sent"]
+
+
+def _count(mask):
+    return bin(mask).count("1")
+
+
+def _ports(topo, here, there):
+    return [c for c in here if all(topo.may_write(c, d) for d in there)]
+
+
+def _send(g, T, topo, core, dests, srcs, dst_ap, sem, alu):
+    mask = topo.mask(core, dests[0])
+    for d in dests:
+        mask &= topo.mask(core, d)
+    ids = []
+    for d in dests:
+        rid, pid, _ = topo.addr(d)
+        ids.append(DstId(rid=rid, pnc=pid))
+    g.remote_dma_fused(
+        [RemoteDMATransfer(dst_ids=ids, dma_engine_mask=mask, remote_sem=sem,
+                           srcs=srcs, dsts=[dst_ap for _ in dests], alu_op=alu)],
+        local_sem=T.sem.sent)
+    return _count(mask)
+
+
+def rank_program(g, core, T, topo):
+    if T.rank_of(core) is None:
+        return
+    cores = list(T.cores)
+    mine = [c for c in cores if topo.chip(c) == topo.chip(core)]
+    far = [c for c in cores if topo.chip(c) != topo.chip(core)]
+    ports = _ports(topo, mine, far)
+    far_ports = _ports(topo, far, mine)
+    k = mine.index(core)
+    peers = [c for c in mine if c != core]
+    first = [c for c in peers if c in ports]
+    later = [c for c in peers if c not in ports]
+    gbuf = [T["g%d" % i] for i in range(len(mine))]
+    arr = [T.sem["arr%d" % i] for i in range(len(mine))]
+    sem = T.sem
+    te, ve, sy, sc = g.tensor, g.vector, g.sync, g.scalar
+
+    sy.dma_start(T.xs[:], T.x[:]).then_inc(sem.ld_x, 16)
+    sc.dma_start(T.xts[:], T.xt[:]).then_inc(sem.ld_xt, 16)
+
+    ve.memset(T.ch[:], -0.5).then_inc(sem.ms, 1)
+    ve.memset(T.c15[:], 1.5).then_inc(sem.ms, 1)
+    ve.wait_ge(sem.s_g, 1)
+    ve.tensor_copy(gbuf[k][:], T.gp[:, 0:D]).then_inc(sem.s_gs, 1)
+    ve.wait_ge(sem.ms, 2)
+    ve.wait_ge(sem.ld_xt, 16)
+    ve.tensor_tensor(T.xth[:], T.xts[:], T.ch[:], AluOpType.mult).then_inc(sem.s_xth, 1)
+    ve.wait_ge(sem.ld_x, 16)
+    ve.tensor_tensor(T.x15[:], T.xs[:], T.c15[:], AluOpType.mult).then_inc(sem.s_x15, 1)
+
+    te.wait_ge(sem.ld_x, 16)
+    te.matmul(T.gp[:, 0:D], T.xs[:], T.xs[:], True, True).then_inc(sem.s_g, 1)
+    te.wait_ge(sem.s_gs, 1)
+    te.wait_ge(sem.s_xth, 1)
+    te.matmul(T.pp[:, 0:D], T.xth[:], gbuf[k][:], True, False)
+    for c in first + later if core in ports else later + first:
+        i = mine.index(c)
+        te.wait_ge(arr[i], _count(topo.mask(c, core)))
+        te.matmul(T.pp[:, 0:D], T.xth[:], gbuf[i][:], False, False)
+    giver = far_ports[k % len(far_ports)]
+    te.wait_ge(sem.arr_x, _count(topo.mask(giver, core)))
+    te.matmul(T.pp[:, 0:D], T.xth[:], T.so[:], False, True).then_inc(sem.s_p, 1)
+
+    sent = 0
+    g.wait_ge(sem.s_gs, 1)
+    if first:
+        sent += _send(g, T, topo, core, first, [gbuf[k][:]], gbuf[k][:], arr[k], 0)
+    if later:
+        sent += _send(g, T, topo, core, later, [gbuf[k][:]], gbuf[k][:], arr[k], 0)
+    if core in ports:
+        for c in peers:
+            g.wait_ge(arr[mine.index(c)], _count(topo.mask(c, core)))
+        j = ports.index(core)
+        share = [d for n, d in enumerate(far) if n % len(ports) == j]
+        sent += _send(g, T, topo, core, share, [b[:] for b in gbuf], T.so[:], sem.arr_x, 1)
+    g.wait_ge(sem.sent, sent)
+
+    ve.wait_ge(sem.s_x15, 1)
+    ve.wait_ge(sem.s_p, 1)
+    ve.tensor_tensor(T.ys[:], T.x15[:], T.pp[:, 0:D], AluOpType.add).then_inc(sem.s_y, 1)
+    sy.wait_ge(sem.s_y, 1)
+    sy.dma_start(T.y[:], T.ys[:]).then_inc(sem.st, 16)
+    sy.wait_ge(sem.st, 16)

@@ -10,16 +10,20 @@ SCRATCH = {
     "c15": ("sbuf", [D, D], F32),
     "xth": ("sbuf", [D, D], F32),
     "x15": ("sbuf", [D, D], F32),
-    "g0": ("sbuf", [D, D], F32),
-    "g1": ("sbuf", [D, D], F32),
-    "g2": ("sbuf", [D, D], F32),
-    "g3": ("sbuf", [D, D], F32),
+    "gs": ("sbuf", [D, D], F32),
+    "l0": ("sbuf", [D, D], F32),
+    "l1": ("sbuf", [D, D], F32),
+    "l2": ("sbuf", [D, D], F32),
+    "l3": ("sbuf", [D, D], F32),
+    "ss": ("sbuf", [D, D], F32),
     "so": ("sbuf", [D, D], F32),
     "ys": ("sbuf", [D, D], F32),
     "gp": ("psum", [D, 512], F32),
+    "qp": ("psum", [D, 512], F32),
+    "aq": ("psum", [D, 512], F32),
     "pp": ("psum", [D, 512], F32),
 }
-SEMAPHORES = ["ld_x", "ld_xt", "ms", "s_g", "s_gs", "s_xth", "s_x15", "s_p", "s_y", "st",
+SEMAPHORES = ["ld_x", "ld_xt", "ms", "s_g", "s_gs", "s_q", "s_a", "s_ss", "s_xth", "s_x15", "s_p", "s_y", "st",
               "arr0", "arr1", "arr2", "arr3", "arr_x", "sent"]
 
 
@@ -31,7 +35,7 @@ def _ports(topo, here, there):
     return [c for c in here if all(topo.may_write(c, d) for d in there)]
 
 
-def _send(g, T, topo, core, dests, srcs, dst_ap, sem, alu):
+def _send(g, T, topo, core, dests, src, dst_ap, sem):
     mask = topo.mask(core, dests[0])
     for d in dests:
         mask &= topo.mask(core, d)
@@ -41,7 +45,7 @@ def _send(g, T, topo, core, dests, srcs, dst_ap, sem, alu):
         ids.append(DstId(rid=rid, pnc=pid))
     g.remote_dma_fused(
         [RemoteDMATransfer(dst_ids=ids, dma_engine_mask=mask, remote_sem=sem,
-                           srcs=srcs, dsts=[dst_ap for _ in dests], alu_op=alu)],
+                           srcs=[src], dsts=[dst_ap for _ in dests], alu_op=0)],
         local_sem=T.sem.sent)
     return _count(mask)
 
@@ -56,56 +60,79 @@ def rank_program(g, core, T, topo):
     far_ports = _ports(topo, far, mine)
     k = mine.index(core)
     peers = [c for c in mine if c != core]
-    first = [c for c in peers if c in ports]
-    later = [c for c in peers if c not in ports]
-    gbuf = [T["g%d" % i] for i in range(len(mine))]
+    p_peers = [c for c in peers if c in ports]
+    n_peers = [c for c in peers if c not in ports]
+    is_port = core in ports
+    land = [T["l%d" % i] for i in range(len(mine))]
     arr = [T.sem["arr%d" % i] for i in range(len(mine))]
     sem = T.sem
     te, ve, sy, sc = g.tensor, g.vector, g.sync, g.scalar
 
+    def landed(q, c):
+        q.wait_ge(arr[mine.index(c)], _count(topo.mask(c, core)))
+
     sy.dma_start(T.xs[:], T.x[:]).then_inc(sem.ld_x, 16)
     sc.dma_start(T.xts[:], T.xt[:]).then_inc(sem.ld_xt, 16)
 
+    sent = 0
+    g.wait_ge(sem.ld_x, 16)
+    if is_port:
+        sent += _send(g, T, topo, core, p_peers, T.xs[:], land[k][:], arr[k])
+        sent += _send(g, T, topo, core, n_peers, T.xs[:], land[k][:], arr[k])
+        g.wait_ge(sem.s_ss, 1)
+        j = ports.index(core)
+        share = [d for n, d in enumerate(far) if n % len(ports) == j]
+        sent += _send(g, T, topo, core, share, T.ss[:], T.so[:], sem.arr_x)
+    else:
+        sent += _send(g, T, topo, core, n_peers, T.xs[:], land[k][:], arr[k])
+        g.wait_ge(sem.s_gs, 1)
+        sent += _send(g, T, topo, core, p_peers, T.gs[:], land[k][:], arr[k])
+    g.wait_ge(sem.sent, sent)
+
+    te.wait_ge(sem.ld_x, 16)
+    if is_port:
+        te.matmul(T.qp[:, 0:D], T.xs[:], T.xs[:], True, False)
+        xk = p_peers
+    else:
+        te.matmul(T.gp[:, 0:D], T.xs[:], T.xs[:], True, True).then_inc(sem.s_g, 1)
+        xk = n_peers + p_peers
+    for n, c in enumerate(xk):
+        landed(te, c)
+        a = land[mine.index(c)]
+        mm = te.matmul(T.qp[:, 0:D], a[:], a[:], (not is_port) and n == 0, n == len(xk) - 1)
+    mm.then_inc(sem.s_q, 1)
+    te.wait_ge(sem.s_xth, 1)
+    te.wait_ge(sem.s_ss, 1)
+    te.matmul(T.pp[:, 0:D], T.xth[:], T.ss[:], True, False)
+    giver = far_ports[k % len(far_ports)]
+    te.wait_ge(sem.arr_x, _count(topo.mask(giver, core)))
+    te.matmul(T.pp[:, 0:D], T.xth[:], T.so[:], False, True).then_inc(sem.s_p, 1)
+
     ve.memset(T.ch[:], -0.5).then_inc(sem.ms, 1)
     ve.memset(T.c15[:], 1.5).then_inc(sem.ms, 1)
-    ve.wait_ge(sem.s_g, 1)
-    ve.tensor_copy(gbuf[k][:], T.gp[:, 0:D]).then_inc(sem.s_gs, 1)
+    if not is_port:
+        ve.wait_ge(sem.s_g, 1)
+        ve.tensor_copy(T.gs[:], T.gp[:, 0:D]).then_inc(sem.s_gs, 1)
     ve.wait_ge(sem.ms, 2)
     ve.wait_ge(sem.ld_xt, 16)
     ve.tensor_tensor(T.xth[:], T.xts[:], T.ch[:], AluOpType.mult).then_inc(sem.s_xth, 1)
     ve.wait_ge(sem.ld_x, 16)
     ve.tensor_tensor(T.x15[:], T.xs[:], T.c15[:], AluOpType.mult).then_inc(sem.s_x15, 1)
-
-    te.wait_ge(sem.ld_x, 16)
-    te.matmul(T.gp[:, 0:D], T.xs[:], T.xs[:], True, True).then_inc(sem.s_g, 1)
-    te.wait_ge(sem.s_gs, 1)
-    te.wait_ge(sem.s_xth, 1)
-    te.matmul(T.pp[:, 0:D], T.xth[:], gbuf[k][:], True, False)
-    for c in first + later if core in ports else later + first:
-        i = mine.index(c)
-        te.wait_ge(arr[i], _count(topo.mask(c, core)))
-        te.matmul(T.pp[:, 0:D], T.xth[:], gbuf[i][:], False, False)
-    giver = far_ports[k % len(far_ports)]
-    te.wait_ge(sem.arr_x, _count(topo.mask(giver, core)))
-    te.matmul(T.pp[:, 0:D], T.xth[:], T.so[:], False, True).then_inc(sem.s_p, 1)
-
-    sent = 0
-    g.wait_ge(sem.s_gs, 1)
-    if first:
-        sent += _send(g, T, topo, core, first, [gbuf[k][:]], gbuf[k][:], arr[k], 0)
-    if later:
-        sent += _send(g, T, topo, core, later, [gbuf[k][:]], gbuf[k][:], arr[k], 0)
-    if core in ports:
-        for c in peers:
-            g.wait_ge(arr[mine.index(c)], _count(topo.mask(c, core)))
-        j = ports.index(core)
-        share = [d for n, d in enumerate(far) if n % len(ports) == j]
-        sent += _send(g, T, topo, core, share, [b[:] for b in gbuf], T.so[:], sem.arr_x, 1)
-    g.wait_ge(sem.sent, sent)
-
+    ve.wait_ge(sem.s_q, 1)
+    if is_port:
+        a, b = [land[mine.index(c)] for c in n_peers]
+        landed(ve, n_peers[0])
+        ve.tensor_tensor(T.aq[:, 0:D], T.qp[:, 0:D], a[:], AluOpType.add).then_inc(sem.s_a, 1)
+        ve.wait_ge(sem.s_a, 1)
+        landed(ve, n_peers[1])
+        ve.tensor_tensor(T.ss[:], T.aq[:, 0:D], b[:], AluOpType.add).then_inc(sem.s_ss, 1)
+    else:
+        ve.wait_ge(sem.s_gs, 1)
+        ve.tensor_tensor(T.ss[:], T.qp[:, 0:D], T.gs[:], AluOpType.add).then_inc(sem.s_ss, 1)
     ve.wait_ge(sem.s_x15, 1)
     ve.wait_ge(sem.s_p, 1)
     ve.tensor_tensor(T.ys[:], T.x15[:], T.pp[:, 0:D], AluOpType.add).then_inc(sem.s_y, 1)
+
     sy.wait_ge(sem.s_y, 1)
     sy.dma_start(T.y[:], T.ys[:]).then_inc(sem.st, 16)
     sy.wait_ge(sem.st, 16)

from concourse.bass import DstId, RemoteDMATransfer
from concourse.mybir import AluOpType

D = 128
F32 = "float32"
SCRATCH = {
    "xs": ("sbuf", [D, D], F32),
    "xts": ("sbuf", [D, D], F32),
    "ch": ("sbuf", [D, D], F32),
    "c15": ("sbuf", [D, D], F32),
    "xth": ("sbuf", [D, D], F32),
    "x15": ("sbuf", [D, D], F32),
    "gs": ("sbuf", [D, D], F32),
    "l0": ("sbuf", [D, D], F32),
    "l1": ("sbuf", [D, D], F32),
    "l2": ("sbuf", [D, D], F32),
    "l3": ("sbuf", [D, D], F32),
    "ss": ("sbuf", [D, D], F32),
    "so": ("sbuf", [D, D], F32),
    "ys": ("sbuf", [D, D], F32),
    "gp": ("psum", [D, 512], F32),
    "qp": ("psum", [D, 512], F32),
    "aq": ("psum", [D, 512], F32),
    "pp": ("psum", [D, 512], F32),
}
SEMAPHORES = ["ld_x", "ld_xt", "ms", "s_g", "s_gs", "s_q", "s_a", "s_ss", "s_xth", "s_x15", "s_p", "s_y", "st",
              "arr0", "arr1", "arr2", "arr3", "arr_x", "sent"]


def _count(mask):
    return bin(mask).count("1")


def _ports(topo, here, there):
    return [c for c in here if all(topo.may_write(c, d) for d in there)]


def _send(g, T, topo, core, dests, src, dst_ap, sem):
    mask = topo.mask(core, dests[0])
    for d in dests:
        mask &= topo.mask(core, d)
    ids = []
    for d in dests:
        rid, pid, _ = topo.addr(d)
        ids.append(DstId(rid=rid, pnc=pid))
    g.remote_dma_fused(
        [RemoteDMATransfer(dst_ids=ids, dma_engine_mask=mask, remote_sem=sem,
                           srcs=[src], dsts=[dst_ap for _ in dests], alu_op=0)],
        local_sem=T.sem.sent)
    return _count(mask)


def rank_program(g, core, T, topo):
    if T.rank_of(core) is None:
        return
    cores = list(T.cores)
    mine = [c for c in cores if topo.chip(c) == topo.chip(core)]
    far = [c for c in cores if topo.chip(c) != topo.chip(core)]
    ports = _ports(topo, mine, far)
    far_ports = _ports(topo, far, mine)
    k = mine.index(core)
    peers = [c for c in mine if c != core]
    p_peers = [c for c in peers if c in ports]
    n_peers = [c for c in peers if c not in ports]
    is_port = core in ports
    land = [T["l%d" % i] for i in range(len(mine))]
    arr = [T.sem["arr%d" % i] for i in range(len(mine))]
    sem = T.sem
    te, ve, sy, sc = g.tensor, g.vector, g.sync, g.scalar

    def landed(q, c):
        q.wait_ge(arr[mine.index(c)], _count(topo.mask(c, core)))

    sy.dma_start(T.xs[:], T.x[:]).then_inc(sem.ld_x, 16)
    sc.dma_start(T.xts[:], T.xt[:]).then_inc(sem.ld_xt, 16)

    sent = 0
    g.wait_ge(sem.ld_x, 16)
    if is_port:
        sent += _send(g, T, topo, core, p_peers, T.xs[:], land[k][:], arr[k])
        sent += _send(g, T, topo, core, n_peers, T.xs[:], land[k][:], arr[k])
        g.wait_ge(sem.s_ss, 1)
        j = ports.index(core)
        share = [d for n, d in enumerate(far) if n % len(ports) == j]
        sent += _send(g, T, topo, core, share, T.ss[:], T.so[:], sem.arr_x)
    else:
        sent += _send(g, T, topo, core, n_peers, T.xs[:], land[k][:], arr[k])
        g.wait_ge(sem.s_gs, 1)
        sent += _send(g, T, topo, core, p_peers, T.gs[:], land[k][:], arr[k])
    g.wait_ge(sem.sent, sent)

    te.wait_ge(sem.ld_x, 16)
    if is_port:
        te.matmul(T.qp[:, 0:D], T.xs[:], T.xs[:], True, False)
        xk = p_peers
    else:
        te.matmul(T.gp[:, 0:D], T.xs[:], T.xs[:], True, True).then_inc(sem.s_g, 1)
        xk = n_peers + p_peers
    for n, c in enumerate(xk):
        landed(te, c)
        a = land[mine.index(c)]
        mm = te.matmul(T.qp[:, 0:D], a[:], a[:], (not is_port) and n == 0, n == len(xk) - 1)
    mm.then_inc(sem.s_q, 1)
    te.wait_ge(sem.s_xth, 1)
    te.wait_ge(sem.s_ss, 1)
    te.matmul(T.pp[:, 0:D], T.xth[:], T.ss[:], True, False)
    giver = far_ports[k % len(far_ports)]
    te.wait_ge(sem.arr_x, _count(topo.mask(giver, core)))
    te.matmul(T.pp[:, 0:D], T.xth[:], T.so[:], False, True).then_inc(sem.s_p, 1)

    ve.memset(T.ch[:], -0.5).then_inc(sem.ms, 1)
    ve.memset(T.c15[:], 1.5).then_inc(sem.ms, 1)
    if not is_port:
        ve.wait_ge(sem.s_g, 1)
        ve.tensor_copy(T.gs[:], T.gp[:, 0:D]).then_inc(sem.s_gs, 1)
    ve.wait_ge(sem.ms, 2)
    ve.wait_ge(sem.ld_xt, 16)
    ve.tensor_tensor(T.xth[:], T.xts[:], T.ch[:], AluOpType.mult).then_inc(sem.s_xth, 1)
    ve.wait_ge(sem.ld_x, 16)
    ve.tensor_tensor(T.x15[:], T.xs[:], T.c15[:], AluOpType.mult).then_inc(sem.s_x15, 1)
    ve.wait_ge(sem.s_q, 1)
    if is_port:
        a, b = [land[mine.index(c)] for c in n_peers]
        landed(ve, n_peers[0])
        ve.tensor_tensor(T.aq[:, 0:D], T.qp[:, 0:D], a[:], AluOpType.add).then_inc(sem.s_a, 1)
        ve.wait_ge(sem.s_a, 1)
        landed(ve, n_peers[1])
        ve.tensor_tensor(T.ss[:], T.aq[:, 0:D], b[:], AluOpType.add).then_inc(sem.s_ss, 1)
    else:
        ve.wait_ge(sem.s_gs, 1)
        ve.tensor_tensor(T.ss[:], T.qp[:, 0:D], T.gs[:], AluOpType.add).then_inc(sem.s_ss, 1)
    ve.wait_ge(sem.s_x15, 1)
    ve.wait_ge(sem.s_p, 1)
    ve.tensor_tensor(T.ys[:], T.x15[:], T.pp[:, 0:D], AluOpType.add).then_inc(sem.s_y, 1)

    sy.wait_ge(sem.s_y, 1)
    sy.dma_start(T.y[:], T.ys[:]).then_inc(sem.st, 16)
    sy.wait_ge(sem.st, 16)
